import numpy as np
import ml_dtypes


def mxq(x, axis, fmt="e4m3"):
    dtype, down = {"e4m3": (ml_dtypes.float8_e4m3fn, 7), "e5m2": (ml_dtypes.float8_e5m2, 14)}[fmt]
    v = np.moveaxis(np.asarray(x, np.float32).astype(ml_dtypes.bfloat16).astype(np.float64), axis, -1)
    blocks = v.reshape(v.shape[:-1] + (-1, 32))
    amax = np.abs(blocks).max(-1, keepdims=True)
    byte = np.maximum(np.where(amax > 0, np.frexp(amax)[1] - 1 + 127, 0) - down, 1)
    scale = np.exp2(byte - 127.0)
    codes = (blocks / scale).astype(np.float32).astype(dtype).astype(np.float64)
    return np.moveaxis((codes * scale).reshape(v.shape), -1, axis)


WIDE = False


def mx_kscale(k):
    if not WIDE:
        return np.ones(k)
    levels = np.array([10, -10, 5, -5, 0])
    if k % 512:
        return np.exp2(np.random.permutation(np.resize(levels, k // 32))).repeat(32)
    a = np.empty((k // 512, 16))
    for p in range(k // 512):
        a[p, :8] = np.random.permutation(np.resize(levels, 8))
        for g in range(8):
            far = levels[np.abs(levels - a[p, g]) >= 10]
            a[p, g + 8] = far[np.random.randint(len(far))]
    return np.exp2(a.ravel()).repeat(32)


def f64(x):
    return np.asarray(x).astype(np.float64)


def striped(idx):
    return np.tile(idx.reshape(-1, 16).T, (8, 1)).astype(np.uint16)


def unstriped(offs):
    return offs[:16].T.reshape(-1).astype(np.int64)


E2M1 = np.array([0.0, 0.5, 1.0, 1.5, 2.0, 3.0, 4.0, 6.0, -0.0, -0.5, -1.0, -1.5, -2.0, -3.0, -4.0, -6.0])


def pack_weight(w, fmt):
    k, n = w.shape
    w = f64(np.asarray(w, np.float32).astype(ml_dtypes.bfloat16)).reshape(k // 32, 32, n)
    amax = np.abs(w).max(1)
    if fmt == "e4m3":
        byte = np.frexp(amax)[1] - 1 + 127 - 7
    else:
        mant, ex = np.frexp(amax / 6.0)
        byte = np.where(mant > 0.5, ex, ex - 1) + 127
    byte = np.clip(np.where(amax > 0, byte, 1), 1, 254)
    scaled = (w * np.exp2(127.0 - byte)[:, None, :]).reshape(k, n).astype(np.float32)
    by_word = np.ascontiguousarray(scaled.reshape(k // 512, 128, 4, n).transpose(0, 1, 3, 2))
    if fmt == "e4m3":
        words = by_word.astype(ml_dtypes.float8_e4m3fn).view(np.uint8)
    else:
        c = by_word.astype(ml_dtypes.float4_e2m1fn).view(np.uint8) & 0xF
        words = (c[..., 0::2] | (c[..., 1::2] << 4)).reshape(k // 512, 128, 2 * n)
    return np.ascontiguousarray(words), np.ascontiguousarray(byte.astype(np.uint8).reshape(k // 512, 16, n))


def unpack_weight(words, scales, fmt):
    g, _, n = scales.shape
    words = np.ascontiguousarray(words).reshape(g, 128, n, -1)
    if fmt == "e4m3":
        vals = words.view(ml_dtypes.float8_e4m3fn).astype(np.float64)
    else:
        nib = np.empty((g, 128, n, 4), np.uint8)
        nib[..., 0::2] = words & 0xF
        nib[..., 1::2] = words >> 4
        vals = E2M1[nib]
    vals = vals * np.repeat(np.exp2(scales.astype(np.float64) - 127.0), 8, axis=1)[..., None]
    return vals.transpose(0, 1, 3, 2).reshape(g * 512, n)


def gelu(v):
    return 0.5 * v * (1.0 + np.tanh(np.sqrt(2.0 / np.pi) * (v + 0.044715 * v**3)))


K, T, S, H, P, N = 1024, 4096, 1024, 1024, 512, 512

def setup_inputs():
    n = np.random.standard_normal
    s = mx_kscale(K)[:, None]
    u = mx_kscale(H)[:, None]
    d = {}
    d["tab_words"], d["tab_scales"] = pack_weight(n((K, T)) * s, "e2m1")
    d["offs"] = striped(np.random.permutation(T)[:S])
    d["pos1"] = striped(np.random.permutation(S)[:P])
    d["pos2"] = striped(np.random.permutation(S)[:P])
    d["w1"] = (1.5 * n((K, H)) / K ** 0.5 / s).astype(np.float32)
    d["lead"] = (0.5 * np.exp(0.3 * n(H)) * u[:, 0]).astype(np.float32)
    d["ref"] = (np.random.uniform(0.2, 1.2, H) * u[:, 0]).astype(np.float32)
    d["w4_words"], d["w4_scales"] = pack_weight(1.5 * n((H, N)) / H ** 0.5 / u, "e2m1")
    return d

def reference(tab_words, tab_scales, offs, pos1, pos2, w1, lead, ref, w4_words, w4_scales):
    v = unpack_weight(tab_words, tab_scales, "e2m1")[:, unstriped(offs)]
    w1q = mxq(f64(w1), 0, "e4m3")
    x = w1q.T @ v
    h = f64(lead)[:, None] * x * (1.0 + np.tanh(0.7978845608 * (x + 0.044715 * x ** 3)))
    day = f64(ref)[:, None]
    painted = np.abs(h[:, unstriped(pos1)] - day)
    natural = np.abs(h[:, unstriped(pos2)] - day)
    z = painted - natural
    zq = mxq(z, 0, "e4m3")
    w4 = unpack_weight(w4_words, w4_scales, "e2m1")
    out = np.tanh(w4.T @ zq)
    return out

@@ -1,0 +1,255 @@
+from contextlib import ExitStack
+
+import concourse.mybir as mybir
+
+K, T, S, H, PAIRS, N = 1024, 4096, 1024, 1024, 512, 512
+FLOPS = 2 * K * H * S + 2 * H * N * PAIRS
+
+F32 = mybir.dt.float32
+BF16 = mybir.dt.bfloat16
+I32 = mybir.dt.int32
+U32 = mybir.dt.uint32
+U16 = mybir.dt.uint16
+U8 = mybir.dt.uint8
+FP8X4 = mybir.dt.float8_e4m3fn_x4
+FP4X4 = mybir.dt.float4_e2m1fn_x4
+ACT = mybir.ActivationFunctionType
+ALU = mybir.AluOpType
+
+P = 128
+PACK = 4
+PASS = P * PACK
+BANK = 512
+LIST = 16
+
+
+def tile_list_iris_repaint_hints_kernel(
+    tc, tab_words, tab_scales, offs, pos1, pos2, w1, lead, ref, w4_words, w4_scales, out
+):
+    nc = tc.nc
+    with ExitStack() as ctx:
+        lists = ctx.enter_context(tc.tile_pool(name="lists", bufs=1))
+        keep = ctx.enter_context(tc.tile_pool(name="keep", bufs=1))
+        psum = ctx.enter_context(tc.psum_pool(name="psum", bufs=1))
+
+        def sb(name, shape, dtype, tag=None):
+            return keep.tile(shape, dtype, name=name, tag=tag or name, align_bytes=64)
+
+        banks = [psum.tile([P, BANK], F32, name=f"bank{i}") for i in range(8)]
+
+        offs_t = lists.tile([P, S // LIST], U16, name="offs_t")
+        pos1_t = lists.tile([P, PAIRS // LIST], U16, name="pos1_t")
+        pos2_t = lists.tile([P, PAIRS // LIST], U16, name="pos2_t")
+        scale_win = sb("scale_win", [P, T], U8)
+        nc.sync.dma_start(offs_t[:], offs)
+        nc.sync.dma_start(
+            scale_win[0:32, :].bitcast(I32), tab_scales.bitcast(I32).rearrange("a q n -> q a n")
+        )
+        nc.sync.dma_start(pos1_t[:], pos1)
+        nc.sync.dma_start(pos2_t[:], pos2)
+        nc.vector.memset(scale_win[32:64, :].bitcast(I32), 0)
+        nc.vector.memset(scale_win[64:128, :].bitcast(I32), 0)
+
+        word_win = [sb(f"word_win{a}", [P, T], U16, tag=f"stage{a}") for a in range(2)]
+        for a in range(2):
+            nc.sync.dma_start(word_win[a][:].bitcast(I32), tab_words[a].bitcast(I32))
+
+        def load_w1(name, a, c0, width, tag=None):
+            raw = sb(name, [P, PACK, width], F32, tag=tag)
+            rows = w1[a * PASS : (a + 1) * PASS, c0 : c0 + width]
+            nc.sync.dma_start(raw[:], rows.rearrange("(p j) c -> p j c", j=PACK))
+            return raw
+
+        head_raw = [[load_w1(f"raw{a}h{h}", a, 256 * h, 256) for h in range(2)] for a in range(2)]
+
+        warm = sb("warm", [P, 2], F32)
+        nc.gpsimd.memset(warm[:, 0:1], 0.0)
+        nc.scalar.activation(warm[:, 1:2], warm[:, 0:1], ACT.Gelu_apprx_tanh)
+
+        lead_t = sb("lead_t", [P, 8], F32)
+        ref_t = sb("ref_t", [P, 8], F32)
+        gain = sb("gain", [P, 8], F32)
+        for tile, vec in ((lead_t, lead), (ref_t, ref)):
+            nc.gpsimd.dma_start(
+                tile[:].rearrange("p (b t) -> p b t", t=PACK), vec.rearrange("(b p t) -> p b t", p=P, t=PACK)
+            )
+        v_planes = sb("v_planes", [P, 2, S], U8)
+        nc.gpsimd.memset(v_planes[:].rearrange("p a n -> p (a n)").bitcast(I32), 0)
+        w4_planes = sb("w4_planes", [P, 2, N], U8)
+        nc.gpsimd.memset(w4_planes[:].rearrange("p a n -> p (a n)").bitcast(I32), 0)
+        nc.gpsimd.tensor_scalar(gain[:], lead_t[:], -2.0, 0.0, ALU.mult, ALU.add)
+        for q in range(4):
+            nc.gpsimd.dma_start(
+                w4_planes[32 * q : 32 * q + 4, :, :].bitcast(I32),
+                w4_scales.bitcast(I32)[:, 4 * q : 4 * q + 4, :].rearrange("a r n -> r a n"),
+            )
+
+        v_scales = sb("v_scales", [P, S], U8)
+        nc.vector.tensor_copy(v_scales[:], scale_win[:].indirect(offs_t[:]))
+        for q in range(4):
+            nc.scalar.dma_start(
+                v_planes[32 * q : 32 * q + 4, :, :].bitcast(I32), v_scales[8 * q : 8 * q + 8, :].bitcast(I32)
+            )
+        v_words = [sb(f"v_words{a}", [P, S], U16) for a in range(2)]
+        for a in range(2):
+            nc.vector.tensor_copy(v_words[a][:], word_win[a][:].indirect(offs_t[:]))
+
+        w_codes = [[sb(f"w_codes{a}{b}", [P, PASS], U32) for b in range(2)] for a in range(2)]
+        w_scales = [[sb(f"w_scales{a}{b}", [P, PASS], U8) for b in range(2)] for a in range(2)]
+        w_bf = [[sb(f"w_bf{a}{b}", [P, PACK, P, PACK], BF16) for b in range(2)] for a in range(2)]
+
+        def cast_w1(copy, a, b, raw, m0):
+            count = raw.shape[2] // PACK
+            copy(
+                w_bf[a][b][:, :, m0 : m0 + count, :].rearrange("p t m j -> p m j t"),
+                raw[:].rearrange("p j (m t) -> p m j t", t=PACK),
+            )
+
+        def quantize_w1(a, b, t0, t1):
+            cols = slice(t0 * P, t1 * P)
+            nc.vector.quantize_mx(
+                out=w_codes[a][b][:, cols].bitcast(FP8X4),
+                scales=w_scales[a][b][:, cols],
+                in_=w_bf[a][b][:, t0:t1, :, :].rearrange("p t m j -> p (t m j)"),
+            )
+
+        cast_w1(nc.scalar.copy, 0, 0, head_raw[0][0], 0)
+        cast_w1(nc.scalar.copy, 0, 0, head_raw[0][1], 64)
+        quantize_w1(0, 0, 0, 4)
+        cast_w1(nc.scalar.copy, 1, 0, head_raw[1][0], 0)
+        cast_w1(nc.vector.tensor_copy, 1, 0, head_raw[1][1], 64)
+        for t in range(PACK):
+            quantize_w1(1, 0, t, t + 1)
+
+        for a in range(2):
+            raw = load_w1(f"raw{a}late", a, PASS, PASS, tag=f"stage{a}")
+            cast_w1(nc.vector.tensor_copy, a, 1, raw, 0)
+            quantize_w1(a, 1, 0, 4)
+        w4_t = sb("w4_t", [P, 2, N], U16, tag="raw0h0")
+        nc.sync.dma_start(w4_t[:].bitcast(I32), w4_words.bitcast(I32).rearrange("a p n -> p a n"))
+
+        gelu = [sb(f"gelu{i}", [P, S], F32) for i in range(2)]
+        dist = [sb(f"dist{i}", [P, S], F32) for i in range(8)]
+
+        def first_stage(i):
+            b, t = divmod(i, PACK)
+            for h in range(2):
+                bank = banks[(2 * i + h) % 8]
+                cols = slice(h * BANK, (h + 1) * BANK)
+                for a in range(2):
+                    nc.tensor.matmul_mx(
+                        out=bank[:],
+                        lhsT=w_codes[a][b][:, t * P : (t + 1) * P].bitcast(FP8X4),
+                        lhsT_scale=w_scales[a][b][:, t * P : (t + 1) * P],
+                        rhs=v_words[a][:, cols].bitcast(FP4X4),
+                        rhs_scale=v_planes[:, a, cols],
+                        start=(a == 0),
+                        stop=(a == 1),
+                    )
+                nc.scalar.activation(gelu[i % 2][:, cols], bank[:], ACT.Gelu_apprx_tanh)
+            nc.scalar.activation(
+                dist[i][:], gelu[i % 2][:], ACT.Abs, bias=ref_t[:, i : i + 1], scale=gain[:, i : i + 1]
+            )
+
+        chunks = [[(0, 256), (256, 256)], [(0, 256), (256, 128), (384, 128)]]
+        z_f32 = [
+            [sb(f"z{b}{c}", [P, PACK, w], F32) for c, (m0, w) in enumerate(chunks[b])] for b in range(2)
+        ]
+
+        def entries(tile, m0, w):
+            return tile[:, m0 // LIST : (m0 + w) // LIST]
+
+        def pick_natural(i, m0, w, dst):
+            nc.vector.tensor_copy(dst, dist[i][:].indirect(entries(pos2_t, m0, w)))
+
+        def pick_painted(i, c, natural):
+            b, t = divmod(i, PACK)
+            m0, w = chunks[b][c]
+            nc.vector.tensor_tensor(
+                z_f32[b][c][:, t, :], dist[i][:].indirect(entries(pos1_t, m0, w)), natural, ALU.subtract
+            )
+
+        natural = [sb(f"natural{i}", [P, PAIRS], F32) for i in range(2)]
+        for i in range(6):
+            first_stage(i)
+            buf = natural[i % 2]
+            for m0 in (0, 256):
+                pick_natural(i, m0, 256, buf[:, m0 : m0 + 256])
+            for c, (m0, w) in enumerate(chunks[i // PACK]):
+                pick_painted(i, c, buf[:, m0 : m0 + w])
+        first_stage(6)
+        first_stage(7)
+
+        z_codes = [sb(f"z_codes{b}", [P, PAIRS], U32) for b in range(2)]
+        z_scales = [sb(f"z_scales{b}", [P, PAIRS], U8) for b in range(2)]
+
+        def interleave(copy, b, c, dst):
+            copy(
+                dst.rearrange("p (c i t) -> p c t i", i=4, t=PACK),
+                z_f32[b][c][:].rearrange("p t (c i) -> p c t i", i=4),
+            )
+
+        def quantize_z(b, m0, w, src):
+            nc.vector.quantize_mx(
+                out=z_codes[b][:, m0 : m0 + w].bitcast(FP8X4), scales=z_scales[b][:, m0 : m0 + w], in_=src
+            )
+
+        def second_stage(b, m0):
+            bank = banks[m0 // P]
+            for nt in range(4):
+                nc.tensor.matmul_mx(
+                    out=bank[:, nt * P : (nt + 1) * P],
+                    lhsT=w4_t[:, b, nt * P : (nt + 1) * P].bitcast(FP4X4),
+                    lhsT_scale=w4_planes[:, b, nt * P : (nt + 1) * P],
+                    rhs=z_codes[b][:, m0 : m0 + P].bitcast(FP8X4),
+                    rhs_scale=z_scales[b][:, m0 : m0 + P],
+                    start=(b == 0 and nt == 0),
+                    stop=(b == 1 and nt == 3),
+                )
+
+        out_v = out.rearrange("(nt p) m -> p nt m", p=P)
+
+        def finish(c):
+            m0, w = chunks[1][c]
+            hints = sb(f"hints{c}", [P, 4, w], F32)
+            for d in range(0, w, P):
+                second_stage(1, m0 + d)
+            for d in range(0, w, P):
+                nc.scalar.activation(
+                    hints[:, :, d : d + P],
+                    banks[(m0 + d) // P][:].rearrange("p (nt m) -> p nt m", m=P),
+                    ACT.Tanh,
+                )
+            nc.sync.dma_start(out_v[:, :, m0 : m0 + w], hints[:])
+
+        def pick_last_two(c, natural7, natural6):
+            m0, w = chunks[1][c]
+            pick_natural(7, m0, w, natural7)
+            pick_natural(6, m0, w, natural6)
+            pick_painted(7, c, natural7)
+            pick_painted(6, c, natural6)
+
+        z0_bf = gelu[0][:].bitcast(BF16)
+        z1_bf = [sb(f"z1_bf{c}", [P, PACK * w], BF16) for c, (m0, w) in enumerate(chunks[1])]
+        n7 = sb("n7", [P, 256], F32)
+        n6 = sb("n6", [P, 256], F32)
+
+        pick_last_two(0, n7[:], n6[:])
+        for c in range(2):
+            interleave(nc.scalar.copy, 0, c, z0_bf[:, 1024 * c : 1024 * (c + 1)])
+        quantize_z(0, 0, PAIRS, z0_bf)
+        for m0 in range(0, PAIRS, P):
+            second_stage(0, m0)
+        interleave(nc.scalar.copy, 1, 0, z1_bf[0][:])
+
+        pick_last_two(1, gelu[0][:, 0:128], n7[:, 0:128])
+        quantize_z(1, 0, 256, z1_bf[0][:])
+        interleave(nc.scalar.copy, 1, 1, z1_bf[1][:])
+
+        pick_last_two(2, z1_bf[0][:].bitcast(F32)[:, 0:128], gelu[0][:, 0:128])
+        quantize_z(1, 256, 128, z1_bf[1][:])
+        interleave(nc.vector.tensor_copy, 1, 2, z1_bf[2][:])
+        finish(0)
+        quantize_z(1, 384, 128, z1_bf[2][:])
+        finish(1)
+        finish(2)

@@ -45,14 +45,14 @@ def tile_list_iris_repaint_hints_kernel(
         nc.sync.dma_start(
             scale_win[0:32, :].bitcast(I32), tab_scales.bitcast(I32).rearrange("a q n -> q a n")
         )
-        nc.sync.dma_start(pos1_t[:], pos1)
-        nc.sync.dma_start(pos2_t[:], pos2)
         nc.vector.memset(scale_win[32:64, :].bitcast(I32), 0)
         nc.vector.memset(scale_win[64:128, :].bitcast(I32), 0)
 
         word_win = [sb(f"word_win{a}", [P, T], U16, tag=f"stage{a}") for a in range(2)]
         for a in range(2):
             nc.sync.dma_start(word_win[a][:].bitcast(I32), tab_words[a].bitcast(I32))
+        nc.sync.dma_start(pos1_t[:], pos1)
+        nc.sync.dma_start(pos2_t[:], pos2)
 
         def load_w1(name, a, c0, width, tag=None):
             raw = sb(name, [P, PACK, width], F32, tag=tag)
@@ -60,7 +60,8 @@ def tile_list_iris_repaint_hints_kernel(
             nc.sync.dma_start(raw[:], rows.rearrange("(p j) c -> p j c", j=PACK))
             return raw
 
-        head_raw = [[load_w1(f"raw{a}h{h}", a, 256 * h, 256) for h in range(2)] for a in range(2)]
+        raw0 = load_w1("raw0", 0, 0, PASS)
+        raw1 = [load_w1(f"raw1h{h}", 1, 256 * h, 256) for h in range(2)]
 
         warm = sb("warm", [P, 2], F32)
         nc.gpsimd.memset(warm[:, 0:1], 0.0)
@@ -75,14 +76,7 @@ def tile_list_iris_repaint_hints_kernel(
             )
         v_planes = sb("v_planes", [P, 2, S], U8)
         nc.gpsimd.memset(v_planes[:].rearrange("p a n -> p (a n)").bitcast(I32), 0)
-        w4_planes = sb("w4_planes", [P, 2, N], U8)
-        nc.gpsimd.memset(w4_planes[:].rearrange("p a n -> p (a n)").bitcast(I32), 0)
         nc.gpsimd.tensor_scalar(gain[:], lead_t[:], -2.0, 0.0, ALU.mult, ALU.add)
-        for q in range(4):
-            nc.gpsimd.dma_start(
-                w4_planes[32 * q : 32 * q + 4, :, :].bitcast(I32),
-                w4_scales.bitcast(I32)[:, 4 * q : 4 * q + 4, :].rearrange("a r n -> r a n"),
-            )
 
         v_scales = sb("v_scales", [P, S], U8)
         nc.vector.tensor_copy(v_scales[:], scale_win[:].indirect(offs_t[:]))
@@ -94,62 +88,85 @@ def tile_list_iris_repaint_hints_kernel(
         for a in range(2):
             nc.vector.tensor_copy(v_words[a][:], word_win[a][:].indirect(offs_t[:]))
 
-        w_codes = [[sb(f"w_codes{a}{b}", [P, PASS], U32) for b in range(2)] for a in range(2)]
+        w_codes = {}
         w_scales = [[sb(f"w_scales{a}{b}", [P, PASS], U8) for b in range(2)] for a in range(2)]
-        w_bf = [[sb(f"w_bf{a}{b}", [P, PACK, P, PACK], BF16) for b in range(2)] for a in range(2)]
+        w_bf = [[sb(f"w_bf{a}0", [P, PACK, P, PACK], BF16), None] for a in range(2)]
 
         def cast_w1(copy, a, b, raw, m0):
             count = raw.shape[2] // PACK
             copy(
                 w_bf[a][b][:, :, m0 : m0 + count, :].rearrange("p t m j -> p m j t"),
-                raw[:].rearrange("p j (m t) -> p m j t", t=PACK),
+                raw.rearrange("p j (m t) -> p m j t", t=PACK),
             )
 
-        def quantize_w1(a, b, t0, t1):
+        def quantize_w1(a, b, t0, t1, tag=None):
             cols = slice(t0 * P, t1 * P)
+            codes = sb(f"w_codes{a}{b}{t0}", [P, (t1 - t0) * P], U32, tag=tag)
+            for t in range(t0, t1):
+                w_codes[a, b, t] = codes[:, (t - t0) * P : (t - t0 + 1) * P]
             nc.vector.quantize_mx(
-                out=w_codes[a][b][:, cols].bitcast(FP8X4),
+                out=codes[:].bitcast(FP8X4),
                 scales=w_scales[a][b][:, cols],
                 in_=w_bf[a][b][:, t0:t1, :, :].rearrange("p t m j -> p (t m j)"),
             )
 
-        cast_w1(nc.scalar.copy, 0, 0, head_raw[0][0], 0)
-        cast_w1(nc.scalar.copy, 0, 0, head_raw[0][1], 64)
-        quantize_w1(0, 0, 0, 4)
-        cast_w1(nc.scalar.copy, 1, 0, head_raw[1][0], 0)
-        cast_w1(nc.vector.tensor_copy, 1, 0, head_raw[1][1], 64)
-        for t in range(PACK):
-            quantize_w1(1, 0, t, t + 1)
+        cast_w1(nc.scalar.copy, 0, 0, raw0[:, :, 0:256], 0)
+        cast_w1(nc.vector.tensor_copy, 0, 0, raw0[:, :, 256:512], 64)
+        quantize_w1(0, 0, 0, 1)
+        cast_w1(nc.scalar.copy, 1, 0, raw1[0][:], 0)
+        cast_w1(nc.vector.tensor_copy, 1, 0, raw1[1][:], 64)
+        quantize_w1(1, 0, 0, 1)
+        quantize_w1(1, 0, 1, 2)
+        quantize_w1(0, 0, 1, 2, tag="raw1h1")
+        quantize_w1(1, 0, 2, 4)
+        quantize_w1(0, 0, 2, 4, tag="raw1h0")
 
-        for a in range(2):
-            raw = load_w1(f"raw{a}late", a, PASS, PASS, tag=f"stage{a}")
-            cast_w1(nc.vector.tensor_copy, a, 1, raw, 0)
-            quantize_w1(a, 1, 0, 4)
-        w4_t = sb("w4_t", [P, 2, N], U16, tag="raw0h0")
+        late_raw = [load_w1(f"raw{a}late", a, PASS, PASS, tag=f"stage{a}") for a in range(2)]
+        w_bf[0][1] = sb("w_bf01", [P, PACK, P, PACK], BF16, tag="w_bf00")
+        cast_w1(nc.vector.tensor_copy, 0, 1, late_raw[0][:], 0)
+        quantize_w1(0, 1, 0, 4)
+        w4_t = sb("w4_t", [P, 2, N], U16, tag="raw0")
         nc.sync.dma_start(w4_t[:].bitcast(I32), w4_words.bitcast(I32).rearrange("a p n -> p a n"))
 
+        w4_planes = sb("w4_planes", [P, 2, N], U8, tag="v_scales")
+        nc.gpsimd.memset(w4_planes[:].rearrange("p a n -> p (a n)").bitcast(I32), 0)
+        for q in range(4):
+            nc.sync.dma_start(
+                w4_planes[32 * q : 32 * q + 4, :, :].bitcast(I32),
+                w4_scales.bitcast(I32)[:, 4 * q : 4 * q + 4, :].rearrange("a r n -> r a n"),
+            )
+
         gelu = [sb(f"gelu{i}", [P, S], F32) for i in range(2)]
+        gelu_first = sb("gelu_first", [P, S], F32)
         dist = [sb(f"dist{i}", [P, S], F32) for i in range(8)]
 
         def first_stage(i):
             b, t = divmod(i, PACK)
+            g = gelu_first if i == 0 else gelu[i % 2]
             for h in range(2):
                 bank = banks[(2 * i + h) % 8]
                 cols = slice(h * BANK, (h + 1) * BANK)
-                for a in range(2):
+                order = (1, 0) if 0 < i < PACK else (0, 1)
+                for a in order:
                     nc.tensor.matmul_mx(
                         out=bank[:],
-                        lhsT=w_codes[a][b][:, t * P : (t + 1) * P].bitcast(FP8X4),
+                        lhsT=w_codes[a, b, t].bitcast(FP8X4),
                         lhsT_scale=w_scales[a][b][:, t * P : (t + 1) * P],
                         rhs=v_words[a][:, cols].bitcast(FP4X4),
                         rhs_scale=v_planes[:, a, cols],
-                        start=(a == 0),
-                        stop=(a == 1),
+                        start=(a == order[0]),
+                        stop=(a == order[1]),
                     )
-                nc.scalar.activation(gelu[i % 2][:, cols], bank[:], ACT.Gelu_apprx_tanh)
-            nc.scalar.activation(
-                dist[i][:], gelu[i % 2][:], ACT.Abs, bias=ref_t[:, i : i + 1], scale=gain[:, i : i + 1]
-            )
+                nc.scalar.activation(g[:, cols], bank[:], ACT.Gelu_apprx_tanh)
+            width = BANK if i in (0, 7) else S
+            for c0 in range(0, S, width):
+                nc.scalar.activation(
+                    dist[i][:, c0 : c0 + width],
+                    g[:, c0 : c0 + width],
+                    ACT.Abs,
+                    bias=ref_t[:, i : i + 1],
+                    scale=gain[:, i : i + 1],
+                )
 
         chunks = [[(0, 256), (256, 256)], [(0, 256), (256, 128), (384, 128)]]
         z_f32 = [
@@ -177,6 +194,10 @@ def tile_list_iris_repaint_hints_kernel(
                 pick_natural(i, m0, 256, buf[:, m0 : m0 + 256])
             for c, (m0, w) in enumerate(chunks[i // PACK]):
                 pick_painted(i, c, buf[:, m0 : m0 + w])
+            if i == 0:
+                w_bf[1][1] = sb("w_bf11", [P, PACK, P, PACK], BF16, tag="gelu_first")
+                cast_w1(nc.vector.tensor_copy, 1, 1, late_raw[1][:], 0)
+                quantize_w1(1, 1, 0, 4)
         first_stage(6)
         first_stage(7)
 
@@ -214,13 +235,15 @@ def tile_list_iris_repaint_hints_kernel(
             hints = sb(f"hints{c}", [P, 4, w], F32)
             for d in range(0, w, P):
                 second_stage(1, m0 + d)
-            for d in range(0, w, P):
-                nc.scalar.activation(
-                    hints[:, :, d : d + P],
-                    banks[(m0 + d) // P][:].rearrange("p (nt m) -> p nt m", m=P),
-                    ACT.Tanh,
-                )
-            nc.sync.dma_start(out_v[:, :, m0 : m0 + w], hints[:])
+            parts = ((0, 2), (2, 4)) if c == 2 else ((0, 4),)
+            for n0, n1 in parts:
+                for d in range(0, w, P):
+                    nc.scalar.activation(
+                        hints[:, n0:n1, d : d + P],
+                        banks[(m0 + d) // P][:, n0 * P : n1 * P].rearrange("p (nt m) -> p nt m", m=P),
+                        ACT.Tanh,
+                    )
+                nc.sync.dma_start(out_v[:, n0:n1, m0 : m0 + w], hints[:, n0:n1, :])
 
         def pick_last_two(c, natural7, natural6):
             m0, w = chunks[1][c]
@@ -235,15 +258,18 @@ def tile_list_iris_repaint_hints_kernel(
         n6 = sb("n6", [P, 256], F32)
 
         pick_last_two(0, n7[:], n6[:])
-        for c in range(2):
-            interleave(nc.scalar.copy, 0, c, z0_bf[:, 1024 * c : 1024 * (c + 1)])
-        quantize_z(0, 0, PAIRS, z0_bf)
-        for m0 in range(0, PAIRS, P):
+        interleave(nc.scalar.copy, 0, 0, z0_bf[:, 0:1024])
+        quantize_z(0, 0, 256, z0_bf[:, 0:1024])
+        for m0 in (0, 128):
             second_stage(0, m0)
+        interleave(nc.scalar.copy, 0, 1, z0_bf[:, 1024:2048])
         interleave(nc.scalar.copy, 1, 0, z1_bf[0][:])
 
         pick_last_two(1, gelu[0][:, 0:128], n7[:, 0:128])
         quantize_z(1, 0, 256, z1_bf[0][:])
+        quantize_z(0, 256, 256, z0_bf[:, 1024:2048])
+        for m0 in (256, 384):
+            second_stage(0, m0)
         interleave(nc.scalar.copy, 1, 1, z1_bf[1][:])
 
         pick_last_two(2, z1_bf[0][:].bitcast(F32)[:, 0:128], gelu[0][:, 0:128])

@@ -19,8 +19,15 @@ ALU = mybir.AluOpType
 P = 128
 PACK = 4
 PASS = P * PACK
+PASSES = 2
+QUADRANTS = 4
 BANK = 512
+BANKS = 8
 LIST = 16
+ROW_TILES = H // P
+OUT_TILES = N // P
+HALF = PASS // 2
+CHUNKS = [[(0, HALF), (HALF, HALF)], [(0, HALF), (HALF, P), (HALF + P, P)]]
 
 
 def tile_list_iris_repaint_hints_kernel(
@@ -35,21 +42,19 @@ def tile_list_iris_repaint_hints_kernel(
         def sb(name, shape, dtype, tag=None):
             return keep.tile(shape, dtype, name=name, tag=tag or name, align_bytes=64)
 
-        banks = [psum.tile([P, BANK], F32, name=f"bank{i}") for i in range(8)]
+        banks = [psum.tile([P, BANK], F32, name=f"bank{i}") for i in range(BANKS)]
 
         offs_t = lists.tile([P, S // LIST], U16, name="offs_t")
         pos1_t = lists.tile([P, PAIRS // LIST], U16, name="pos1_t")
         pos2_t = lists.tile([P, PAIRS // LIST], U16, name="pos2_t")
         scale_win = sb("scale_win", [P, T], U8)
         nc.sync.dma_start(offs_t[:], offs)
-        nc.sync.dma_start(
-            scale_win[0:32, :].bitcast(I32), tab_scales.bitcast(I32).rearrange("a q n -> q a n")
-        )
+        nc.sync.dma_start(scale_win[0:32, :].bitcast(I32), tab_scales.bitcast(I32).rearrange("a q n -> q a n"))
         nc.vector.memset(scale_win[32:64, :].bitcast(I32), 0)
         nc.vector.memset(scale_win[64:128, :].bitcast(I32), 0)
 
-        word_win = [sb(f"word_win{a}", [P, T], U16, tag=f"stage{a}") for a in range(2)]
-        for a in range(2):
+        word_win = [sb(f"word_win{a}", [P, T], U16, tag=f"stage{a}") for a in range(PASSES)]
+        for a in range(PASSES):
             nc.sync.dma_start(word_win[a][:].bitcast(I32), tab_words[a].bitcast(I32))
         nc.sync.dma_start(pos1_t[:], pos1)
         nc.sync.dma_start(pos2_t[:], pos2)
@@ -61,90 +66,88 @@ def tile_list_iris_repaint_hints_kernel(
             return raw
 
         raw0 = load_w1("raw0", 0, 0, PASS)
-        raw1 = [load_w1(f"raw1h{h}", 1, 256 * h, 256) for h in range(2)]
+        raw1 = [load_w1(f"raw1h{h}", 1, h * HALF, HALF) for h in range(2)]
 
-        warm = sb("warm", [P, 2], F32)
-        nc.gpsimd.memset(warm[:, 0:1], 0.0)
-        nc.scalar.activation(warm[:, 1:2], warm[:, 0:1], ACT.Gelu_apprx_tanh)
-
-        lead_t = sb("lead_t", [P, 8], F32)
-        ref_t = sb("ref_t", [P, 8], F32)
-        gain = sb("gain", [P, 8], F32)
+        lead_t = sb("lead_t", [P, ROW_TILES], F32)
+        ref_t = sb("ref_t", [P, ROW_TILES], F32)
+        gain = sb("gain", [P, ROW_TILES], F32)
         for tile, vec in ((lead_t, lead), (ref_t, ref)):
             nc.gpsimd.dma_start(
                 tile[:].rearrange("p (b t) -> p b t", t=PACK), vec.rearrange("(b p t) -> p b t", p=P, t=PACK)
             )
-        v_planes = sb("v_planes", [P, 2, S], U8)
+        v_planes = sb("v_planes", [P, PASSES, S], U8)
         nc.gpsimd.memset(v_planes[:].rearrange("p a n -> p (a n)").bitcast(I32), 0)
         nc.gpsimd.tensor_scalar(gain[:], lead_t[:], -2.0, 0.0, ALU.mult, ALU.add)
 
         v_scales = sb("v_scales", [P, S], U8)
         nc.vector.tensor_copy(v_scales[:], scale_win[:].indirect(offs_t[:]))
-        for q in range(4):
+        for quad in range(QUADRANTS):
             nc.scalar.dma_start(
-                v_planes[32 * q : 32 * q + 4, :, :].bitcast(I32), v_scales[8 * q : 8 * q + 8, :].bitcast(I32)
+                v_planes[32 * quad : 32 * quad + 4, :, :].bitcast(I32),
+                v_scales[8 * quad : 8 * quad + 8, :].bitcast(I32),
             )
-        v_words = [sb(f"v_words{a}", [P, S], U16) for a in range(2)]
-        for a in range(2):
+        v_words = [sb(f"v_words{a}", [P, S], U16) for a in range(PASSES)]
+        for a in range(PASSES):
             nc.vector.tensor_copy(v_words[a][:], word_win[a][:].indirect(offs_t[:]))
 
         w_codes = {}
-        w_scales = [[sb(f"w_scales{a}{b}", [P, PASS], U8) for b in range(2)] for a in range(2)]
-        w_bf = [[sb(f"w_bf{a}0", [P, PACK, P, PACK], BF16), None] for a in range(2)]
+        w_scales = [[sb(f"w_scales{a}{b}", [P, PASS], U8) for b in range(PASSES)] for a in range(PASSES)]
+        w_bf = {(a, 0): sb(f"w_bf{a}0", [P, PACK, P, PACK], BF16) for a in range(PASSES)}
 
         def cast_w1(copy, a, b, raw, m0):
             count = raw.shape[2] // PACK
             copy(
-                w_bf[a][b][:, :, m0 : m0 + count, :].rearrange("p t m j -> p m j t"),
+                w_bf[a, b][:, :, m0 : m0 + count, :].rearrange("p t m j -> p m j t"),
                 raw.rearrange("p j (m t) -> p m j t", t=PACK),
             )
 
         def quantize_w1(a, b, t0, t1, tag=None):
-            cols = slice(t0 * P, t1 * P)
             codes = sb(f"w_codes{a}{b}{t0}", [P, (t1 - t0) * P], U32, tag=tag)
             for t in range(t0, t1):
                 w_codes[a, b, t] = codes[:, (t - t0) * P : (t - t0 + 1) * P]
             nc.vector.quantize_mx(
                 out=codes[:].bitcast(FP8X4),
-                scales=w_scales[a][b][:, cols],
-                in_=w_bf[a][b][:, t0:t1, :, :].rearrange("p t m j -> p (t m j)"),
+                scales=w_scales[a][b][:, t0 * P : t1 * P],
+                in_=w_bf[a, b][:, t0:t1, :, :].rearrange("p t m j -> p (t m j)"),
             )
 
-        cast_w1(nc.scalar.copy, 0, 0, raw0[:, :, 0:256], 0)
-        cast_w1(nc.vector.tensor_copy, 0, 0, raw0[:, :, 256:512], 64)
+        half_m = HALF // PACK
+        cast_w1(nc.scalar.copy, 0, 0, raw0[:, :, 0:HALF], 0)
+        cast_w1(nc.vector.tensor_copy, 0, 0, raw0[:, :, HALF:PASS], half_m)
         quantize_w1(0, 0, 0, 1)
         cast_w1(nc.scalar.copy, 1, 0, raw1[0][:], 0)
-        cast_w1(nc.vector.tensor_copy, 1, 0, raw1[1][:], 64)
+        cast_w1(nc.vector.tensor_copy, 1, 0, raw1[1][:], half_m)
         quantize_w1(1, 0, 0, 1)
         quantize_w1(1, 0, 1, 2)
         quantize_w1(0, 0, 1, 2, tag="raw1h1")
-        quantize_w1(1, 0, 2, 4)
-        quantize_w1(0, 0, 2, 4, tag="raw1h0")
+        quantize_w1(1, 0, 2, PACK)
+        quantize_w1(0, 0, 2, PACK, tag="raw1h0")
 
-        late_raw = [load_w1(f"raw{a}late", a, PASS, PASS, tag=f"stage{a}") for a in range(2)]
-        w_bf[0][1] = sb("w_bf01", [P, PACK, P, PACK], BF16, tag="w_bf00")
+        late_raw = [load_w1(f"raw{a}late", a, PASS, PASS, tag=f"stage{a}") for a in range(PASSES)]
+        w_bf[0, 1] = sb("w_bf01", [P, PACK, P, PACK], BF16, tag="w_bf00")
         cast_w1(nc.vector.tensor_copy, 0, 1, late_raw[0][:], 0)
-        quantize_w1(0, 1, 0, 4)
-        w4_t = sb("w4_t", [P, 2, N], U16, tag="raw0")
-        nc.sync.dma_start(w4_t[:].bitcast(I32), w4_words.bitcast(I32).rearrange("a p n -> p a n"))
+        quantize_w1(0, 1, 0, PACK)
 
-        w4_planes = sb("w4_planes", [P, 2, N], U8, tag="v_scales")
+        w4_t = sb("w4_t", [P, PASSES, N], U16, tag="raw0")
+        nc.sync.dma_start(w4_t[:].bitcast(I32), w4_words.bitcast(I32).rearrange("a p n -> p a n"))
+        w4_planes = sb("w4_planes", [P, PASSES, N], U8, tag="v_scales")
         nc.gpsimd.memset(w4_planes[:].rearrange("p a n -> p (a n)").bitcast(I32), 0)
-        for q in range(4):
+        for quad in range(QUADRANTS):
             nc.sync.dma_start(
-                w4_planes[32 * q : 32 * q + 4, :, :].bitcast(I32),
-                w4_scales.bitcast(I32)[:, 4 * q : 4 * q + 4, :].rearrange("a r n -> r a n"),
+                w4_planes[32 * quad : 32 * quad + 4, :, :].bitcast(I32),
+                w4_scales.bitcast(I32)[:, 4 * quad : 4 * quad + 4, :].rearrange("a r n -> r a n"),
             )
 
         gelu = [sb(f"gelu{i}", [P, S], F32) for i in range(2)]
         gelu_first = sb("gelu_first", [P, S], F32)
-        dist = [sb(f"dist{i}", [P, S], F32) for i in range(8)]
+        dist = [sb(f"dist{i}", [P, S], F32) for i in range(ROW_TILES)]
+        tile6, tile7 = ROW_TILES - 2, ROW_TILES - 1
 
         def first_stage(i):
             b, t = divmod(i, PACK)
             g = gelu_first if i == 0 else gelu[i % 2]
-            for h in range(2):
-                bank = banks[(2 * i + h) % 8]
+            for h in range(S // BANK):
+                bank = banks[(2 * i + h) % BANKS]
                 cols = slice(h * BANK, (h + 1) * BANK)
                 order = (1, 0) if 0 < i < PACK else (0, 1)
                 for a in order:
@@ -158,7 +161,7 @@ def tile_list_iris_repaint_hints_kernel(
                         stop=(a == order[1]),
                     )
                 nc.scalar.activation(g[:, cols], bank[:], ACT.Gelu_apprx_tanh)
-            width = BANK if i in (0, 7) else S
+            width = BANK if i in (0, tile7) else S
             for c0 in range(0, S, width):
                 nc.scalar.activation(
                     dist[i][:, c0 : c0 + width],
@@ -168,9 +171,8 @@ def tile_list_iris_repaint_hints_kernel(
                     scale=gain[:, i : i + 1],
                 )
 
-        chunks = [[(0, 256), (256, 256)], [(0, 256), (256, 128), (384, 128)]]
         z_f32 = [
-            [sb(f"z{b}{c}", [P, PACK, w], F32) for c, (m0, w) in enumerate(chunks[b])] for b in range(2)
+            [sb(f"z{b}{c}", [P, PACK, w], F32) for c, (m0, w) in enumerate(CHUNKS[b])] for b in range(PASSES)
         ]
 
         def entries(tile, m0, w):
@@ -179,64 +181,68 @@ def tile_list_iris_repaint_hints_kernel(
         def pick_natural(i, m0, w, dst):
             nc.vector.tensor_copy(dst, dist[i][:].indirect(entries(pos2_t, m0, w)))
 
-        def pick_painted(i, c, natural):
+        def pick_painted(i, c, src):
             b, t = divmod(i, PACK)
-            m0, w = chunks[b][c]
+            m0, w = CHUNKS[b][c]
             nc.vector.tensor_tensor(
-                z_f32[b][c][:, t, :], dist[i][:].indirect(entries(pos1_t, m0, w)), natural, ALU.subtract
+                z_f32[b][c][:, t, :], dist[i][:].indirect(entries(pos1_t, m0, w)), src, ALU.subtract
             )
 
         natural = [sb(f"natural{i}", [P, PAIRS], F32) for i in range(2)]
-        for i in range(6):
+        for i in range(tile6):
             first_stage(i)
             buf = natural[i % 2]
-            for m0 in (0, 256):
-                pick_natural(i, m0, 256, buf[:, m0 : m0 + 256])
-            for c, (m0, w) in enumerate(chunks[i // PACK]):
+            for m0 in (0, HALF):
+                pick_natural(i, m0, HALF, buf[:, m0 : m0 + HALF])
+            for c, (m0, w) in enumerate(CHUNKS[i // PACK]):
                 pick_painted(i, c, buf[:, m0 : m0 + w])
             if i == 0:
-                w_bf[1][1] = sb("w_bf11", [P, PACK, P, PACK], BF16, tag="gelu_first")
+                w_bf[1, 1] = sb("w_bf11", [P, PACK, P, PACK], BF16, tag="gelu_first")
                 cast_w1(nc.vector.tensor_copy, 1, 1, late_raw[1][:], 0)
-                quantize_w1(1, 1, 0, 4)
-        first_stage(6)
-        first_stage(7)
+                quantize_w1(1, 1, 0, PACK)
+        first_stage(tile6)
+        first_stage(tile7)
 
-        z_codes = [sb(f"z_codes{b}", [P, PAIRS], U32) for b in range(2)]
-        z_scales = [sb(f"z_scales{b}", [P, PAIRS], U8) for b in range(2)]
+        z_codes = [sb(f"z_codes{b}", [P, PAIRS], U32) for b in range(PASSES)]
+        z_scales = [sb(f"z_scales{b}", [P, PAIRS], U8) for b in range(PASSES)]
 
         def interleave(copy, b, c, dst):
             copy(
-                dst.rearrange("p (c i t) -> p c t i", i=4, t=PACK),
-                z_f32[b][c][:].rearrange("p t (c i) -> p c t i", i=4),
+                dst.rearrange("p (g i t) -> p g t i", i=4, t=PACK),
+                z_f32[b][c][:].rearrange("p t (g i) -> p g t i", i=4),
             )
 
-        def quantize_z(b, m0, w, src):
+        def quantize_z(b, c, src):
+            m0, w = CHUNKS[b][c]
             nc.vector.quantize_mx(
                 out=z_codes[b][:, m0 : m0 + w].bitcast(FP8X4), scales=z_scales[b][:, m0 : m0 + w], in_=src
             )
 
-        def second_stage(b, m0):
-            bank = banks[m0 // P]
-            for nt in range(4):
-                nc.tensor.matmul_mx(
-                    out=bank[:, nt * P : (nt + 1) * P],
-                    lhsT=w4_t[:, b, nt * P : (nt + 1) * P].bitcast(FP4X4),
-                    lhsT_scale=w4_planes[:, b, nt * P : (nt + 1) * P],
-                    rhs=z_codes[b][:, m0 : m0 + P].bitcast(FP8X4),
-                    rhs_scale=z_scales[b][:, m0 : m0 + P],
-                    start=(b == 0 and nt == 0),
-                    stop=(b == 1 and nt == 3),
-                )
+        def second_stage(b, c):
+            first, w = CHUNKS[b][c]
+            for m0 in range(first, first + w, P):
+                bank = banks[m0 // P]
+                for nt in range(OUT_TILES):
+                    nc.tensor.matmul_mx(
+                        out=bank[:, nt * P : (nt + 1) * P],
+                        lhsT=w4_t[:, b, nt * P : (nt + 1) * P].bitcast(FP4X4),
+                        lhsT_scale=w4_planes[:, b, nt * P : (nt + 1) * P],
+                        rhs=z_codes[b][:, m0 : m0 + P].bitcast(FP8X4),
+                        rhs_scale=z_scales[b][:, m0 : m0 + P],
+                        start=(b == 0 and nt == 0),
+                        stop=(b == 1 and nt == OUT_TILES - 1),
+                    )
 
         out_v = out.rearrange("(nt p) m -> p nt m", p=P)
+        last = len(CHUNKS[1]) - 1
 
         def finish(c):
-            m0, w = chunks[1][c]
-            hints = sb(f"hints{c}", [P, 4, w], F32)
-            for d in range(0, w, P):
-                second_stage(1, m0 + d)
-            parts = ((0, 2), (2, 4)) if c == 2 else ((0, 4),)
-            for n0, n1 in parts:
+            m0, w = CHUNKS[1][c]
+            hints = sb(f"hints{c}", [P, OUT_TILES, w], F32)
+            second_stage(1, c)
+            step = OUT_TILES // 2 if c == last else OUT_TILES
+            for n0 in range(0, OUT_TILES, step):
+                n1 = n0 + step
                 for d in range(0, w, P):
                     nc.scalar.activation(
                         hints[:, n0:n1, d : d + P],
@@ -246,36 +252,34 @@ def tile_list_iris_repaint_hints_kernel(
                 nc.sync.dma_start(out_v[:, n0:n1, m0 : m0 + w], hints[:, n0:n1, :])
 
         def pick_last_two(c, natural7, natural6):
-            m0, w = chunks[1][c]
-            pick_natural(7, m0, w, natural7)
-            pick_natural(6, m0, w, natural6)
-            pick_painted(7, c, natural7)
-            pick_painted(6, c, natural6)
+            m0, w = CHUNKS[1][c]
+            pick_natural(tile7, m0, w, natural7)
+            pick_natural(tile6, m0, w, natural6)
+            pick_painted(tile7, c, natural7)
+            pick_painted(tile6, c, natural6)
 
-        z0_bf = gelu[0][:].bitcast(BF16)
-        z1_bf = [sb(f"z1_bf{c}", [P, PACK * w], BF16) for c, (m0, w) in enumerate(chunks[1])]
-        n7 = sb("n7", [P, 256], F32)
-        n6 = sb("n6", [P, 256], F32)
+        z0_bf = [gelu[0][:].bitcast(BF16)[:, PACK * m0 : PACK * (m0 + w)] for m0, w in CHUNKS[0]]
+        z1_bf = [sb(f"z1_bf{c}", [P, PACK * w], BF16) for c, (m0, w) in enumerate(CHUNKS[1])]
+        n7 = sb("n7", [P, HALF], F32)
+        n6 = sb("n6", [P, HALF], F32)
 
         pick_last_two(0, n7[:], n6[:])
-        interleave(nc.scalar.copy, 0, 0, z0_bf[:, 0:1024])
-        quantize_z(0, 0, 256, z0_bf[:, 0:1024])
-        for m0 in (0, 128):
-            second_stage(0, m0)
-        interleave(nc.scalar.copy, 0, 1, z0_bf[:, 1024:2048])
+        interleave(nc.scalar.copy, 0, 0, z0_bf[0])
+        quantize_z(0, 0, z0_bf[0])
+        second_stage(0, 0)
+        interleave(nc.scalar.copy, 0, 1, z0_bf[1])
         interleave(nc.scalar.copy, 1, 0, z1_bf[0][:])
 
-        pick_last_two(1, gelu[0][:, 0:128], n7[:, 0:128])
-        quantize_z(1, 0, 256, z1_bf[0][:])
-        quantize_z(0, 256, 256, z0_bf[:, 1024:2048])
-        for m0 in (256, 384):
-            second_stage(0, m0)
+        pick_last_two(1, gelu[0][:, 0:P], n7[:, 0:P])
+        quantize_z(1, 0, z1_bf[0][:])
+        quantize_z(0, 1, z0_bf[1])
+        second_stage(0, 1)
         interleave(nc.scalar.copy, 1, 1, z1_bf[1][:])
 
-        pick_last_two(2, z1_bf[0][:].bitcast(F32)[:, 0:128], gelu[0][:, 0:128])
-        quantize_z(1, 256, 128, z1_bf[1][:])
+        pick_last_two(2, z1_bf[0][:].bitcast(F32)[:, 0:P], gelu[0][:, 0:P])
+        quantize_z(1, 1, z1_bf[1][:])
         interleave(nc.vector.tensor_copy, 1, 2, z1_bf[2][:])
         finish(0)
-        quantize_z(1, 384, 128, z1_bf[2][:])
+        quantize_z(1, 2, z1_bf[2][:])
         finish(1)
         finish(2)

from contextlib import ExitStack

import concourse.mybir as mybir

K, T, S, H, PAIRS, N = 1024, 4096, 1024, 1024, 512, 512
FLOPS = 2 * K * H * S + 2 * H * N * PAIRS

F32 = mybir.dt.float32
BF16 = mybir.dt.bfloat16
I32 = mybir.dt.int32
U32 = mybir.dt.uint32
U16 = mybir.dt.uint16
U8 = mybir.dt.uint8
FP8X4 = mybir.dt.float8_e4m3fn_x4
FP4X4 = mybir.dt.float4_e2m1fn_x4
ACT = mybir.ActivationFunctionType
ALU = mybir.AluOpType

P = 128
PACK = 4
PASS = P * PACK
PASSES = 2
QUADRANTS = 4
BANK = 512
BANKS = 8
LIST = 16
ROW_TILES = H // P
OUT_TILES = N // P
HALF = PASS // 2
CHUNKS = [[(0, HALF), (HALF, HALF)], [(0, HALF), (HALF, P), (HALF + P, P)]]


def tile_list_iris_repaint_hints_kernel(
    tc, tab_words, tab_scales, offs, pos1, pos2, w1, lead, ref, w4_words, w4_scales, out
):
    nc = tc.nc
    with ExitStack() as ctx:
        lists = ctx.enter_context(tc.tile_pool(name="lists", bufs=1))
        keep = ctx.enter_context(tc.tile_pool(name="keep", bufs=1))
        psum = ctx.enter_context(tc.psum_pool(name="psum", bufs=1))

        def sb(name, shape, dtype, tag=None):
            return keep.tile(shape, dtype, name=name, tag=tag or name, align_bytes=64)

        banks = [psum.tile([P, BANK], F32, name=f"bank{i}") for i in range(BANKS)]

        offs_t = lists.tile([P, S // LIST], U16, name="offs_t")
        pos1_t = lists.tile([P, PAIRS // LIST], U16, name="pos1_t")
        pos2_t = lists.tile([P, PAIRS // LIST], U16, name="pos2_t")
        scale_win = sb("scale_win", [P, T], U8)
        nc.sync.dma_start(offs_t[:], offs)
        nc.sync.dma_start(scale_win[0:32, :].bitcast(I32), tab_scales.bitcast(I32).rearrange("a q n -> q a n"))
        nc.vector.memset(scale_win[32:64, :].bitcast(I32), 0)
        nc.vector.memset(scale_win[64:128, :].bitcast(I32), 0)

        word_win = [sb(f"word_win{a}", [P, T], U16, tag=f"stage{a}") for a in range(PASSES)]
        for a in range(PASSES):
            nc.sync.dma_start(word_win[a][:].bitcast(I32), tab_words[a].bitcast(I32))
        nc.sync.dma_start(pos1_t[:], pos1)
        nc.sync.dma_start(pos2_t[:], pos2)

        def load_w1(name, a, c0, width, tag=None):
            raw = sb(name, [P, PACK, width], F32, tag=tag)
            rows = w1[a * PASS : (a + 1) * PASS, c0 : c0 + width]
            nc.sync.dma_start(raw[:], rows.rearrange("(p j) c -> p j c", j=PACK))
            return raw

        raw0 = load_w1("raw0", 0, 0, PASS)
        raw1 = [load_w1(f"raw1h{h}", 1, h * HALF, HALF) for h in range(2)]

        lead_t = sb("lead_t", [P, ROW_TILES], F32)
        ref_t = sb("ref_t", [P, ROW_TILES], F32)
        gain = sb("gain", [P, ROW_TILES], F32)
        for tile, vec in ((lead_t, lead), (ref_t, ref)):
            nc.gpsimd.dma_start(
                tile[:].rearrange("p (b t) -> p b t", t=PACK), vec.rearrange("(b p t) -> p b t", p=P, t=PACK)
            )
        v_planes = sb("v_planes", [P, PASSES, S], U8)
        nc.gpsimd.memset(v_planes[:].rearrange("p a n -> p (a n)").bitcast(I32), 0)
        nc.gpsimd.tensor_scalar(gain[:], lead_t[:], -2.0, 0.0, ALU.mult, ALU.add)

        v_scales = sb("v_scales", [P, S], U8)
        nc.vector.tensor_copy(v_scales[:], scale_win[:].indirect(offs_t[:]))
        for quad in range(QUADRANTS):
            nc.scalar.dma_start(
                v_planes[32 * quad : 32 * quad + 4, :, :].bitcast(I32),
                v_scales[8 * quad : 8 * quad + 8, :].bitcast(I32),
            )
        v_words = [sb(f"v_words{a}", [P, S], U16) for a in range(PASSES)]
        for a in range(PASSES):
            nc.vector.tensor_copy(v_words[a][:], word_win[a][:].indirect(offs_t[:]))

        w_codes = {}
        w_scales = [[sb(f"w_scales{a}{b}", [P, PASS], U8) for b in range(PASSES)] for a in range(PASSES)]
        w_bf = {(a, 0): sb(f"w_bf{a}0", [P, PACK, P, PACK], BF16) for a in range(PASSES)}

        def cast_w1(copy, a, b, raw, m0):
            count = raw.shape[2] // PACK
            copy(
                w_bf[a, b][:, :, m0 : m0 + count, :].rearrange("p t m j -> p m j t"),
                raw.rearrange("p j (m t) -> p m j t", t=PACK),
            )

        def quantize_w1(a, b, t0, t1, tag=None):
            codes = sb(f"w_codes{a}{b}{t0}", [P, (t1 - t0) * P], U32, tag=tag)
            for t in range(t0, t1):
                w_codes[a, b, t] = codes[:, (t - t0) * P : (t - t0 + 1) * P]
            nc.vector.quantize_mx(
                out=codes[:].bitcast(FP8X4),
                scales=w_scales[a][b][:, t0 * P : t1 * P],
                in_=w_bf[a, b][:, t0:t1, :, :].rearrange("p t m j -> p (t m j)"),
            )

        half_m = HALF // PACK
        cast_w1(nc.scalar.copy, 0, 0, raw0[:, :, 0:HALF], 0)
        cast_w1(nc.vector.tensor_copy, 0, 0, raw0[:, :, HALF:PASS], half_m)
        quantize_w1(0, 0, 0, 1)
        cast_w1(nc.scalar.copy, 1, 0, raw1[0][:], 0)
        cast_w1(nc.vector.tensor_copy, 1, 0, raw1[1][:], half_m)
        quantize_w1(1, 0, 0, 1)
        quantize_w1(1, 0, 1, 2)
        quantize_w1(0, 0, 1, 2, tag="raw1h1")
        quantize_w1(1, 0, 2, PACK)
        quantize_w1(0, 0, 2, PACK, tag="raw1h0")

        late_raw = [load_w1(f"raw{a}late", a, PASS, PASS, tag=f"stage{a}") for a in range(PASSES)]
        w_bf[0, 1] = sb("w_bf01", [P, PACK, P, PACK], BF16, tag="w_bf00")
        cast_w1(nc.vector.tensor_copy, 0, 1, late_raw[0][:], 0)
        quantize_w1(0, 1, 0, PACK)

        w4_t = sb("w4_t", [P, PASSES, N], U16, tag="raw0")
        nc.sync.dma_start(w4_t[:].bitcast(I32), w4_words.bitcast(I32).rearrange("a p n -> p a n"))
        w4_planes = sb("w4_planes", [P, PASSES, N], U8, tag="v_scales")
        nc.gpsimd.memset(w4_planes[:].rearrange("p a n -> p (a n)").bitcast(I32), 0)
        for quad in range(QUADRANTS):
            nc.sync.dma_start(
                w4_planes[32 * quad : 32 * quad + 4, :, :].bitcast(I32),
                w4_scales.bitcast(I32)[:, 4 * quad : 4 * quad + 4, :].rearrange("a r n -> r a n"),
            )

        gelu = [sb(f"gelu{i}", [P, S], F32) for i in range(2)]
        gelu_first = sb("gelu_first", [P, S], F32)
        dist = [sb(f"dist{i}", [P, S], F32) for i in range(ROW_TILES)]
        tile6, tile7 = ROW_TILES - 2, ROW_TILES - 1

        def first_stage(i):
            b, t = divmod(i, PACK)
            g = gelu_first if i == 0 else gelu[i % 2]
            for h in range(S // BANK):
                bank = banks[(2 * i + h) % BANKS]
                cols = slice(h * BANK, (h + 1) * BANK)
                order = (1, 0) if 0 < i < PACK else (0, 1)
                for a in order:
                    nc.tensor.matmul_mx(
                        out=bank[:],
                        lhsT=w_codes[a, b, t].bitcast(FP8X4),
                        lhsT_scale=w_scales[a][b][:, t * P : (t + 1) * P],
                        rhs=v_words[a][:, cols].bitcast(FP4X4),
                        rhs_scale=v_planes[:, a, cols],
                        start=(a == order[0]),
                        stop=(a == order[1]),
                    )
                nc.scalar.activation(g[:, cols], bank[:], ACT.Gelu_apprx_tanh)
            width = BANK if i in (0, tile7) else S
            for c0 in range(0, S, width):
                nc.scalar.activation(
                    dist[i][:, c0 : c0 + width],
                    g[:, c0 : c0 + width],
                    ACT.Abs,
                    bias=ref_t[:, i : i + 1],
                    scale=gain[:, i : i + 1],
                )

        z_f32 = [
            [sb(f"z{b}{c}", [P, PACK, w], F32) for c, (m0, w) in enumerate(CHUNKS[b])] for b in range(PASSES)
        ]

        def entries(tile, m0, w):
            return tile[:, m0 // LIST : (m0 + w) // LIST]

        def pick_natural(i, m0, w, dst):
            nc.vector.tensor_copy(dst, dist[i][:].indirect(entries(pos2_t, m0, w)))

        def pick_painted(i, c, src):
            b, t = divmod(i, PACK)
            m0, w = CHUNKS[b][c]
            nc.vector.tensor_tensor(
                z_f32[b][c][:, t, :], dist[i][:].indirect(entries(pos1_t, m0, w)), src, ALU.subtract
            )

        natural = [sb(f"natural{i}", [P, PAIRS], F32) for i in range(2)]
        for i in range(tile6):
            first_stage(i)
            buf = natural[i % 2]
            for m0 in (0, HALF):
                pick_natural(i, m0, HALF, buf[:, m0 : m0 + HALF])
            for c, (m0, w) in enumerate(CHUNKS[i // PACK]):
                pick_painted(i, c, buf[:, m0 : m0 + w])
            if i == 0:
                w_bf[1, 1] = sb("w_bf11", [P, PACK, P, PACK], BF16, tag="gelu_first")
                cast_w1(nc.vector.tensor_copy, 1, 1, late_raw[1][:], 0)
                quantize_w1(1, 1, 0, PACK)
        first_stage(tile6)
        first_stage(tile7)

        z_codes = [sb(f"z_codes{b}", [P, PAIRS], U32) for b in range(PASSES)]
        z_scales = [sb(f"z_scales{b}", [P, PAIRS], U8) for b in range(PASSES)]

        def interleave(copy, b, c, dst):
            copy(
                dst.rearrange("p (g i t) -> p g t i", i=4, t=PACK),
                z_f32[b][c][:].rearrange("p t (g i) -> p g t i", i=4),
            )

        def quantize_z(b, c, src):
            m0, w = CHUNKS[b][c]
            nc.vector.quantize_mx(
                out=z_codes[b][:, m0 : m0 + w].bitcast(FP8X4), scales=z_scales[b][:, m0 : m0 + w], in_=src
            )

        def second_stage(b, c):
            first, w = CHUNKS[b][c]
            for m0 in range(first, first + w, P):
                bank = banks[m0 // P]
                for nt in range(OUT_TILES):
                    nc.tensor.matmul_mx(
                        out=bank[:, nt * P : (nt + 1) * P],
                        lhsT=w4_t[:, b, nt * P : (nt + 1) * P].bitcast(FP4X4),
                        lhsT_scale=w4_planes[:, b, nt * P : (nt + 1) * P],
                        rhs=z_codes[b][:, m0 : m0 + P].bitcast(FP8X4),
                        rhs_scale=z_scales[b][:, m0 : m0 + P],
                        start=(b == 0 and nt == 0),
                        stop=(b == 1 and nt == OUT_TILES - 1),
                    )

        out_v = out.rearrange("(nt p) m -> p nt m", p=P)
        last = len(CHUNKS[1]) - 1

        def finish(c):
            m0, w = CHUNKS[1][c]
            hints = sb(f"hints{c}", [P, OUT_TILES, w], F32)
            second_stage(1, c)
            step = OUT_TILES // 2 if c == last else OUT_TILES
            for n0 in range(0, OUT_TILES, step):
                n1 = n0 + step
                for d in range(0, w, P):
                    nc.scalar.activation(
                        hints[:, n0:n1, d : d + P],
                        banks[(m0 + d) // P][:, n0 * P : n1 * P].rearrange("p (nt m) -> p nt m", m=P),
                        ACT.Tanh,
                    )
                nc.sync.dma_start(out_v[:, n0:n1, m0 : m0 + w], hints[:, n0:n1, :])

        def pick_last_two(c, natural7, natural6):
            m0, w = CHUNKS[1][c]
            pick_natural(tile7, m0, w, natural7)
            pick_natural(tile6, m0, w, natural6)
            pick_painted(tile7, c, natural7)
            pick_painted(tile6, c, natural6)

        z0_bf = [gelu[0][:].bitcast(BF16)[:, PACK * m0 : PACK * (m0 + w)] for m0, w in CHUNKS[0]]
        z1_bf = [sb(f"z1_bf{c}", [P, PACK * w], BF16) for c, (m0, w) in enumerate(CHUNKS[1])]
        n7 = sb("n7", [P, HALF], F32)
        n6 = sb("n6", [P, HALF], F32)

        pick_last_two(0, n7[:], n6[:])
        interleave(nc.scalar.copy, 0, 0, z0_bf[0])
        quantize_z(0, 0, z0_bf[0])
        second_stage(0, 0)
        interleave(nc.scalar.copy, 0, 1, z0_bf[1])
        interleave(nc.scalar.copy, 1, 0, z1_bf[0][:])

        pick_last_two(1, gelu[0][:, 0:P], n7[:, 0:P])
        quantize_z(1, 0, z1_bf[0][:])
        quantize_z(0, 1, z0_bf[1])
        second_stage(0, 1)
        interleave(nc.scalar.copy, 1, 1, z1_bf[1][:])

        pick_last_two(2, z1_bf[0][:].bitcast(F32)[:, 0:P], gelu[0][:, 0:P])
        quantize_z(1, 1, z1_bf[1][:])
        interleave(nc.vector.tensor_copy, 1, 2, z1_bf[2][:])
        finish(0)
        quantize_z(1, 2, z1_bf[2][:])
        finish(1)
        finish(2)
